import numpy as np
import ml_dtypes


def mxq(x, axis, fmt="e4m3"):
    dtype, down = {"e4m3": (ml_dtypes.float8_e4m3fn, 7), "e5m2": (ml_dtypes.float8_e5m2, 14)}[fmt]
    v = np.moveaxis(np.asarray(x, np.float32).astype(ml_dtypes.bfloat16).astype(np.float64), axis, -1)
    blocks = v.reshape(v.shape[:-1] + (-1, 32))
    amax = np.abs(blocks).max(-1, keepdims=True)
    byte = np.maximum(np.where(amax > 0, np.frexp(amax)[1] - 1 + 127, 0) - down, 1)
    scale = np.exp2(byte - 127.0)
    codes = (blocks / scale).astype(np.float32).astype(dtype).astype(np.float64)
    return np.moveaxis((codes * scale).reshape(v.shape), -1, axis)


WIDE = False


def mx_kscale(k):
    if not WIDE:
        return np.ones(k)
    levels = np.array([10, -10, 5, -5, 0])
    if k % 512:
        return np.exp2(np.random.permutation(np.resize(levels, k // 32))).repeat(32)
    a = np.empty((k // 512, 16))
    for p in range(k // 512):
        a[p, :8] = np.random.permutation(np.resize(levels, 8))
        for g in range(8):
            far = levels[np.abs(levels - a[p, g]) >= 10]
            a[p, g + 8] = far[np.random.randint(len(far))]
    return np.exp2(a.ravel()).repeat(32)


BF16 = ml_dtypes.bfloat16


def bf(x):
    return np.asarray(x, np.float32).astype(BF16)


def f64(x):
    return np.asarray(x).astype(np.float64)


E2M1 = np.array([0.0, 0.5, 1.0, 1.5, 2.0, 3.0, 4.0, 6.0, -0.0, -0.5, -1.0, -1.5, -2.0, -3.0, -4.0, -6.0])


def pack_weight(w, fmt):
    k, n = w.shape
    w = f64(bf(w)).reshape(k // 32, 32, n)
    amax = np.abs(w).max(1)
    if fmt == "e4m3":
        byte = np.frexp(amax)[1] - 1 + 127 - 7
    else:
        mant, ex = np.frexp(amax / 6.0)
        byte = np.where(mant > 0.5, ex, ex - 1) + 127
    byte = np.clip(np.where(amax > 0, byte, 1), 1, 254)
    scaled = (w * np.exp2(127.0 - byte)[:, None, :]).reshape(k, n).astype(np.float32)
    by_word = np.ascontiguousarray(scaled.reshape(k // 512, 128, 4, n).transpose(0, 1, 3, 2))
    if fmt == "e4m3":
        words = by_word.astype(ml_dtypes.float8_e4m3fn).view(np.uint8)
    else:
        c = by_word.astype(ml_dtypes.float4_e2m1fn).view(np.uint8) & 0xF
        words = c[..., 0::2] | (c[..., 1::2] << 4)
    return np.ascontiguousarray(words), np.ascontiguousarray(byte.astype(np.uint8).reshape(k // 512, 16, n))


def unpack_weight(words, scales, fmt):
    g, p, n, _ = words.shape
    if fmt == "e4m3":
        vals = np.ascontiguousarray(words).view(ml_dtypes.float8_e4m3fn).astype(np.float64)
    else:
        nib = np.empty((g, p, n, 4), np.uint8)
        nib[..., 0::2] = words & 0xF
        nib[..., 1::2] = words >> 4
        vals = E2M1[nib]
    vals = vals * np.repeat(np.exp2(scales.astype(np.float64) - 127.0), 8, axis=1)[..., None]
    return vals.transpose(0, 1, 3, 2).reshape(g * 512, n)
def pack4(w):
    words, scales = pack_weight(w, "e2m1")
    return words.reshape(words.shape[0], 128, -1), scales


def unpack4(words, scales):
    return unpack_weight(words.reshape(words.shape[0], 128, -1, 2), scales, "e2m1")


G, K, V, R = 1024, 512, 2048, 512


def setup_inputs():
    s = mx_kscale(K)
    t = mx_kscale(G)
    basis = np.random.standard_normal((K, R)) / np.sqrt(K) * G ** -0.25
    basis_words, basis_scales = pack4(basis / s[:, None])
    return {
        "design": bf(np.random.standard_normal((G, K)) * s),
        "coef": bf(0.5 * np.random.standard_normal((K, V)) / np.sqrt(K) / s[:, None]),
        "basis_words": basis_words,
        "basis_scales": basis_scales,
        "logsig": bf(np.random.standard_normal((G, V)) * G ** -0.25 * t[:, None]),
        "prec": bf(np.exp(0.3 * np.random.standard_normal(G)) / t),
    }


def reference(design, coef, basis_words, basis_scales, logsig, prec):
    x = mxq(f64(design), 1, "e4m3")
    w = np.exp(x @ mxq(f64(coef), 0, "e4m3"))
    z = w * f64(logsig)
    h = (x @ unpack4(basis_words, basis_scales)) * f64(prec)[:, None]
    return mxq(h, 0, "e4m3").T @ mxq(z, 0, "e4m3")

@@ -1,0 +1,337 @@
+from contextlib import ExitStack
+
+import concourse.mybir as mybir
+from concourse.masks import make_identity
+
+G, K, V, R = 1024, 512, 2048, 512
+FLOPS = 2 * G * K * V + 2 * G * K * R + 2 * G * R * V
+
+F32 = mybir.dt.float32
+BF16 = mybir.dt.bfloat16
+I32 = mybir.dt.int32
+U32 = mybir.dt.uint32
+U8 = mybir.dt.uint8
+FP8X4 = mybir.dt.float8_e4m3fn_x4
+FP4X4 = mybir.dt.float4_e2m1fn_x4
+ACT = mybir.ActivationFunctionType
+ALU = mybir.AluOpType
+
+P = 128
+PACK = 4
+PASSES = G // (P * PACK)
+W = 256
+CHUNKS = V // W
+LOAD_W = 512
+RUN = 4
+
+
+def tile_diffusion_weighted_refit_s11_kernel(tc, design, coef, basis_words, basis_scales, logsig, prec, out):
+    nc = tc.nc
+    with ExitStack() as ctx:
+        keep = ctx.enter_context(tc.tile_pool(name="keep", bufs=1))
+        work = ctx.enter_context(tc.tile_pool(name="work", bufs=3))
+        psum = ctx.enter_context(tc.psum_pool(name="psum", bufs=4))
+        ctx.enter_context(tc.manual_schedule())
+
+        x_rows = design.rearrange("(g p t) k -> g p t k", p=P, t=PACK)
+        c_rows = coef.rearrange("(p t) v -> p t v", t=PACK)
+        y_rows = logsig.rearrange("(g p t) v -> g p t v", p=P, t=PACK)
+        out_rows = out.rearrange("(j p) v -> p j v", p=P)
+
+        warm = keep.tile([P, 1], F32, name="warm")
+        warm_out = keep.tile([P, 1], F32, name="warm_out")
+        nc.vector.memset(warm[:], 0.0)
+        nc.scalar.activation(out=warm_out[:], in_=warm[:], func=ACT.Exp)
+
+        u_scales = keep.tile([P, R], U8, name="u_scales", align_bytes=64)
+        nc.vector.memset(u_scales[:].bitcast(I32), 0)
+        ident = keep.tile([P, P], F32, name="ident")
+        make_identity(nc, ident[:])
+        r_sb = keep.tile([P, PASSES, PACK], BF16, name="r_sb")
+
+        x_raw, c_raw, y_raw = {}, {}, {}
+
+        def load_x(g, h0, n):
+            t = keep.tile([P, 2 * n * K], BF16, name="x_raw%d%d" % (g, h0))
+            nc.sync.dma_start(out=t[:], in_=x_rows[g, :, 2 * h0 : 2 * (h0 + n), :].rearrange("p t k -> p (t k)"))
+            for i in range(n):
+                x_raw[g, h0 + i] = t[:, 2 * K * i : 2 * K * (i + 1)]
+
+        def load_c(c0, n):
+            t = keep.tile([P, PACK, n * W], BF16, name="c_raw%d" % c0)
+            nc.sync.dma_start(out=t[:], in_=c_rows[:, :, c0 * W : (c0 + n) * W])
+            for i in range(n):
+                c_raw[c0 + i] = t[:, :, i * W : (i + 1) * W]
+
+        def load_y(g, c0, n):
+            t = keep.tile([P, PACK, n * W], BF16, name="y_raw%d%d" % (g, c0))
+            nc.sync.dma_start(out=t[:], in_=y_rows[g, :, :, c0 * W : (c0 + n) * W])
+            for i in range(n):
+                y_raw[g, c0 + i] = t[:, :, i * W : (i + 1) * W]
+
+        u_words = keep.tile([P, 2 * R], U8, name="u_words", align_bytes=64)
+
+        load_x(0, 0, 1)
+        load_x(0, 1, 1)
+        for q in range(4):
+            nc.sync.dma_start(
+                out=u_scales[32 * q : 32 * q + 4, :].bitcast(I32),
+                in_=basis_scales[0, 4 * q : 4 * q + 4, :].bitcast(I32),
+            )
+        load_c(0, 1)
+        nc.sync.dma_start(out=u_words[:].bitcast(I32), in_=basis_words[0].bitcast(I32))
+        nc.sync.dma_start(out=r_sb[:], in_=prec.rearrange("(g p t) -> p g t", p=P, t=PACK))
+        load_c(1, 1)
+        load_y(0, 0, 2)
+        load_x(1, 0, 2)
+        load_c(2, 2)
+        load_y(1, 0, 2)
+        load_c(4, 4)
+        load_y(0, 2, 2)
+        load_y(1, 2, 2)
+        load_y(0, 4, 4)
+        load_y(1, 4, 4)
+
+        x_bank, x_grp, x_q, c_grp, c_q = {}, {}, {}, {}, {}
+        s_bank, e_sb, z_grp, z_q, h_bank, h_q, o_bank = {}, {}, {}, {}, {}, {}, {}
+        h_grp = [keep.tile([P, R * PACK], BF16, name="h_grp%d" % g, align_bytes=64) for g in range(PASSES)]
+
+        def quantize(pool, name, tag, src, bufs):
+            n = src.shape[1] // PACK
+            codes = pool.tile([P, n], U32, name=name + "_codes", tag=tag + "_codes", bufs=bufs, align_bytes=64)
+            scales = pool.tile([P, n], U8, name=name + "_scales", tag=tag + "_scales", bufs=bufs, align_bytes=64)
+            nc.vector.quantize_mx(out=codes[:].bitcast(FP8X4), scales=scales[:], in_=src)
+            return codes, scales
+
+        def turn_x(g, h):
+            bank = psum.tile([P, 2, 2, P], F32, name="x_bank", tag="side")
+            words = x_raw[g, h].bitcast(F32)
+            for s in range(2):
+                for u in range(2):
+                    nc.tensor.transpose(bank[:, s, u, :], words[:, 256 * s + u : 256 * (s + 1) : 2], ident[:])
+            x_bank[g, h] = bank
+
+        def copy_x(g, h):
+            t = work.tile([P, 2 * P * PACK], BF16, name="x_grp", align_bytes=64, bufs=4)
+            nc.scalar.copy(
+                out=t[:].bitcast(F32).rearrange("p (s m u) -> p s m u", s=2, u=2),
+                in_=x_bank[g, h][:].rearrange("p s u m -> p s m u"),
+            )
+            x_grp[g, h] = t
+
+        def quant_x(g, h):
+            x_q[g, h] = quantize(keep, "x%d%d" % (g, h), "x%d%d" % (g, h), x_grp[g, h][:], 1)
+
+        def x_slot(g, t):
+            codes, scales = x_q[g, t // 2]
+            cols = slice((t % 2) * P, (t % 2 + 1) * P)
+            return codes[:, cols].bitcast(FP8X4), scales[:, cols]
+
+        def weave_c(c, on_scalar):
+            t = work.tile([P, W * PACK], BF16, name="c_grp", align_bytes=64, bufs=4)
+            dst = t[:].rearrange("p (c i t) -> p c t i", i=RUN, t=PACK)
+            src = c_raw[c].rearrange("p t (c i) -> p c t i", i=RUN)
+            if on_scalar:
+                nc.scalar.copy(out=dst, in_=src)
+            else:
+                nc.vector.tensor_copy(out=dst, in_=src)
+            c_grp[c] = t
+
+        def quant_c(c):
+            c_q[c] = quantize(keep, "c%d" % c, "c%d" % c, c_grp[c][:], 1)
+
+        def mm_s(g, c, h):
+            bank = psum.tile([P, 2, W], F32, name="s_bank", tag="s")
+            codes, scales = c_q[c]
+            for s in range(2):
+                xc, xs = x_slot(g, 2 * h + s)
+                nc.tensor.matmul_mx(
+                    out=bank[:, s, :], lhsT=xc, lhsT_scale=xs, rhs=codes[:].bitcast(FP8X4), rhs_scale=scales[:],
+                    start=True, stop=True,
+                )
+            s_bank[g, c, h] = bank
+
+        def exp_s(g, c, h):
+            if h == 0:
+                e_sb[g, c] = work.tile([P, PACK, W], F32, name="e_sb", bufs=6)
+            nc.scalar.activation(out=e_sb[g, c][:, 2 * h : 2 * h + 2, :], in_=s_bank[g, c, h][:], func=ACT.Exp)
+
+        def mult_z(g, c):
+            t = work.tile([P, W * PACK], BF16, name="z_grp", align_bytes=64)
+            nc.vector.tensor_tensor(
+                out=t[:].rearrange("p (c i t) -> p c t i", i=RUN, t=PACK),
+                in0=e_sb[g, c][:].rearrange("p t (c i) -> p c t i", i=RUN),
+                in1=y_raw[g, c].rearrange("p t (c i) -> p c t i", i=RUN),
+                op=ALU.mult,
+            )
+            z_grp[g, c] = t
+
+        def quant_z(g, c):
+            z_q[g, c] = quantize(work, "z", "z", z_grp[g, c][:], 8)
+
+        def mm_h(g, j):
+            bank = psum.tile([P, PACK, P], F32, name="h_bank", tag="side")
+            for t in range(PACK):
+                xc, xs = x_slot(g, t)
+                nc.tensor.matmul_mx(
+                    out=bank[:, t, :], lhsT=xc, lhsT_scale=xs,
+                    rhs=u_words[:, 2 * P * j : 2 * P * (j + 1)].bitcast(FP4X4),
+                    rhs_scale=u_scales[:, P * j : P * (j + 1)],
+                    start=True, stop=True,
+                )
+            h_bank[g, j] = bank
+
+        def scale_h(g, j):
+            nc.vector.tensor_tensor(
+                out=h_grp[g][:, j * P * PACK : (j + 1) * P * PACK].rearrange("p (n t) -> p n t", t=PACK),
+                in0=h_bank[g, j][:].rearrange("p t n -> p n t"),
+                in1=r_sb[:, g : g + 1, :].to_broadcast([P, P, PACK]),
+                op=ALU.mult,
+            )
+
+        def quant_h(g):
+            h_q[g] = quantize(keep, "h%d" % g, "h%d" % g, h_grp[g][:], 1)
+
+        def mm_o(c):
+            for b in range(2):
+                bank = psum.tile([P, 2, W], F32, name="o_bank", tag="side")
+                for s in range(2):
+                    cols = slice((2 * b + s) * P, (2 * b + s + 1) * P)
+                    for g in range(PASSES):
+                        hc, hs = h_q[g]
+                        zc, zs = z_q[g, c]
+                        nc.tensor.matmul_mx(
+                            out=bank[:, s, :], lhsT=hc[:, cols].bitcast(FP8X4), lhsT_scale=hs[:, cols],
+                            rhs=zc[:].bitcast(FP8X4), rhs_scale=zs[:],
+                            start=(g == 0), stop=(g == PASSES - 1),
+                        )
+                o_bank[c, b] = bank
+
+        def store_o(c, b, on_scalar):
+            t = work.tile([P, 2, W], F32, name="o_sb", bufs=4)
+            if on_scalar:
+                nc.scalar.copy(out=t[:], in_=o_bank[c, b][:])
+            else:
+                nc.vector.tensor_copy(out=t[:], in_=o_bank[c, b][:])
+            nc.sync.dma_start(out=out_rows[:, 2 * b : 2 * b + 2, c * W : (c + 1) * W], in_=t[:])
+
+        def mm_o_last(c, g):
+            for j in range(4):
+                if g == 0:
+                    o_bank[c, j] = psum.tile([P, 2, W], F32, name="o_last", tag="s")
+                cols = slice(j * P, (j + 1) * P)
+                hc, hs = h_q[g]
+                zc, zs = z_q[g, c]
+                nc.tensor.matmul_mx(
+                    out=o_bank[c, j][:, 0, :], lhsT=hc[:, cols].bitcast(FP8X4), lhsT_scale=hs[:, cols],
+                    rhs=zc[:].bitcast(FP8X4), rhs_scale=zs[:],
+                    start=(g == 0), stop=(g == PASSES - 1),
+                )
+
+        def store_last(c, b):
+            t = work.tile([P, 2, W], F32, name="o_sb", bufs=4)
+            nc.scalar.copy(out=t[:, 0, :], in_=o_bank[c, 2 * b][:, 0, :])
+            nc.vector.tensor_copy(out=t[:, 1, :], in_=o_bank[c, 2 * b + 1][:, 0, :])
+            nc.sync.dma_start(out=out_rows[:, 2 * b : 2 * b + 2, c * W : (c + 1) * W], in_=t[:])
+
+        units = [(0, 0), (0, 1), (1, 0), (1, 1)] + [(g, c) for c in range(2, CHUNKS) for g in range(PASSES)]
+
+        def stage_one(k):
+            mm_s(*units[k], 0)
+            mm_s(*units[k], 1)
+
+        def exps(k):
+            exp_s(*units[k], 0)
+            exp_s(*units[k], 1)
+
+        turn_x(0, 0)
+        copy_x(0, 0)
+        turn_x(0, 1)
+        copy_x(0, 1)
+        quant_x(0, 0)
+        weave_c(0, False)
+        quant_x(0, 1)
+        quant_c(0)
+        weave_c(1, True)
+        mm_h(0, 0)
+        stage_one(0)
+        exps(0)
+        mm_h(0, 1)
+        scale_h(0, 0)
+        quant_c(1)
+        stage_one(1)
+        exps(1)
+        scale_h(0, 1)
+        mm_h(0, 2)
+        mm_h(0, 3)
+        mult_z(*units[0])
+        turn_x(1, 0)
+        turn_x(1, 1)
+        copy_x(1, 0)
+        copy_x(1, 1)
+        scale_h(0, 2)
+        scale_h(0, 3)
+        quant_z(*units[0])
+        quant_x(1, 0)
+        quant_x(1, 1)
+        weave_c(2, True)
+        stage_one(2)
+        mm_h(1, 0)
+        mm_h(1, 1)
+        stage_one(3)
+        mm_h(1, 2)
+        mm_h(1, 3)
+        exps(2)
+        weave_c(3, True)
+        exps(3)
+        mult_z(*units[1])
+        quant_h(0)
+        quant_c(2)
+        stage_one(4)
+        scale_h(1, 0)
+        scale_h(1, 1)
+        quant_z(*units[1])
+        scale_h(1, 2)
+        scale_h(1, 3)
+        mult_z(*units[2])
+        quant_h(1)
+        quant_c(3)
+        weave_c(4, True)
+        exps(4)
+        stage_one(5)
+        quant_z(*units[2])
+
+        last = len(units) - 1
+        pending = []
+        for k in range(3, last):
+            if k + 2 <= last:
+                exps(k + 2)
+            if k + 3 <= last:
+                stage_one(k + 3)
+            if k > 3 and units[k - 1][0] == PASSES - 1:
+                quant_z(*units[k - 1])
+            if units[k - 1][0] == PASSES - 1:
+                mm_o(units[k - 1][1])
+                pending.extend([(units[k - 1][1], 0), (units[k - 1][1], 1)])
+            if k == 3:
+                weave_c(5, True)
+            for n in range(2 if k in (5, 7) else 1):
+                if k > 3:
+                    store_o(*pending[0], True)
+                    pending.remove(pending[0])
+            mult_z(*units[k])
+            if k > 3 and units[k - 1][0] != PASSES - 1:
+                quant_z(*units[k - 1])
+            if k in (3, 5, 7, 9):
+                quant_c(k // 2 + 3)
+            if k in (6, 8):
+                weave_c(k // 2 + 3, False)
+        quant_z(*units[last - 1])
+        mm_o_last(CHUNKS - 1, 0)
+        for c, b in pending:
+            store_o(c, b, True)
+        mult_z(*units[last])
+        quant_z(*units[last])
+        mm_o_last(CHUNKS - 1, 1)
+        store_last(CHUNKS - 1, 0)
+        store_last(CHUNKS - 1, 1)

@@ -21,7 +21,9 @@ PACK = 4
 PASSES = G // (P * PACK)
 W = 256
 CHUNKS = V // W
-LOAD_W = 512
+BANK = 512
+WARM1 = 10
+WARM2 = 4
 RUN = 4
 
 
@@ -38,18 +40,18 @@ def tile_diffusion_weighted_refit_s11_kernel(tc, design, coef, basis_words, basi
         y_rows = logsig.rearrange("(g p t) v -> g p t v", p=P, t=PACK)
         out_rows = out.rearrange("(j p) v -> p j v", p=P)
 
-        warm = keep.tile([P, 1], F32, name="warm")
+        zeros = keep.tile([P, P * PACK], BF16, name="zeros", align_bytes=64)
         warm_out = keep.tile([P, 1], F32, name="warm_out")
-        nc.vector.memset(warm[:], 0.0)
-        nc.scalar.activation(out=warm_out[:], in_=warm[:], func=ACT.Exp)
 
         u_scales = keep.tile([P, R], U8, name="u_scales", align_bytes=64)
         nc.vector.memset(u_scales[:].bitcast(I32), 0)
+        nc.vector.memset(zeros[:], 0.0)
+        nc.scalar.activation(out=warm_out[:], in_=zeros[:, 0:1], func=ACT.Exp)
         ident = keep.tile([P, P], F32, name="ident")
         make_identity(nc, ident[:])
         r_sb = keep.tile([P, PASSES, PACK], BF16, name="r_sb")
 
-        x_raw, c_raw, y_raw = {}, {}, {}
+        x_raw, c_raw, y_raw = {}, {}, [{}, {}]
 
         def load_x(g, h0, n):
             t = keep.tile([P, 2 * n * K], BF16, name="x_raw%d%d" % (g, h0))
@@ -57,51 +59,69 @@ def tile_diffusion_weighted_refit_s11_kernel(tc, design, coef, basis_words, basi
             for i in range(n):
                 x_raw[g, h0 + i] = t[:, 2 * K * i : 2 * K * (i + 1)]
 
-        def load_c(c0, n):
-            t = keep.tile([P, PACK, n * W], BF16, name="c_raw%d" % c0)
-            nc.sync.dma_start(out=t[:], in_=c_rows[:, :, c0 * W : (c0 + n) * W])
-            for i in range(n):
-                c_raw[c0 + i] = t[:, :, i * W : (i + 1) * W]
+        def load_c(v0, w):
+            t = keep.tile([P, PACK, w], BF16, name="c_raw%d" % v0)
+            nc.sync.dma_start(out=t[:], in_=c_rows[:, :, v0 : v0 + w])
+            c_raw[v0, v0 + w] = t
 
-        def load_y(g, c0, n):
-            t = keep.tile([P, PACK, n * W], BF16, name="y_raw%d%d" % (g, c0))
-            nc.sync.dma_start(out=t[:], in_=y_rows[g, :, :, c0 * W : (c0 + n) * W])
-            for i in range(n):
-                y_raw[g, c0 + i] = t[:, :, i * W : (i + 1) * W]
+        def load_y(g, v0, w):
+            t = keep.tile([P, PACK, w], BF16, name="y_raw%d_%d" % (g, v0))
+            nc.sync.dma_start(out=t[:], in_=y_rows[g, :, :, v0 : v0 + w])
+            y_raw[g][v0, v0 + w] = t
+
+        def window(loaded, v0, w):
+            for (lo, hi), t in loaded.items():
+                if lo <= v0 and v0 + w <= hi:
+                    return t[:, :, v0 - lo : v0 - lo + w]
+            raise ValueError("columns not loaded")
 
         u_words = keep.tile([P, 2 * R], U8, name="u_words", align_bytes=64)
 
         load_x(0, 0, 1)
-        load_x(0, 1, 1)
         for q in range(4):
             nc.sync.dma_start(
                 out=u_scales[32 * q : 32 * q + 4, :].bitcast(I32),
                 in_=basis_scales[0, 4 * q : 4 * q + 4, :].bitcast(I32),
             )
-        load_c(0, 1)
+        load_x(0, 1, 1)
+        load_c(0, 256)
         nc.sync.dma_start(out=u_words[:].bitcast(I32), in_=basis_words[0].bitcast(I32))
+        load_c(256, 256)
         nc.sync.dma_start(out=r_sb[:], in_=prec.rearrange("(g p t) -> p g t", p=P, t=PACK))
-        load_c(1, 1)
-        load_y(0, 0, 2)
+        load_y(0, 0, 512)
         load_x(1, 0, 2)
-        load_c(2, 2)
-        load_y(1, 0, 2)
-        load_c(4, 4)
-        load_y(0, 2, 2)
-        load_y(1, 2, 2)
-        load_y(0, 4, 4)
-        load_y(1, 4, 4)
+        load_c(512, 512)
+        load_y(1, 0, 512)
+        load_y(0, 512, 512)
+        load_c(1024, 1024)
+        load_y(1, 512, 512)
+        load_y(0, 1024, 1024)
+        load_y(1, 1024, 1024)
 
-        x_bank, x_grp, x_q, c_grp, c_q = {}, {}, {}, {}, {}
-        s_bank, e_sb, z_grp, z_q, h_bank, h_q, o_bank = {}, {}, {}, {}, {}, {}, {}
-        h_grp = [keep.tile([P, R * PACK], BF16, name="h_grp%d" % g, align_bytes=64) for g in range(PASSES)]
+        x_bank, s_banks, e_sb, z_grp, h_bank, o_bank = {}, {}, {}, {}, {}, {}
 
-        def quantize(pool, name, tag, src, bufs):
-            n = src.shape[1] // PACK
-            codes = pool.tile([P, n], U32, name=name + "_codes", tag=tag + "_codes", bufs=bufs, align_bytes=64)
-            scales = pool.tile([P, n], U8, name=name + "_scales", tag=tag + "_scales", bufs=bufs, align_bytes=64)
-            nc.vector.quantize_mx(out=codes[:].bitcast(FP8X4), scales=scales[:], in_=src)
+        def mx_tiles(name, n):
+            codes = keep.tile([P, n], U32, name=name + "_codes", align_bytes=64)
+            scales = keep.tile([P, n], U8, name=name + "_scales", align_bytes=64)
             return codes, scales
+
+        def mx_cols(tiles, c0, n):
+            return tiles[0][:, c0 : c0 + n].bitcast(FP8X4), tiles[1][:, c0 : c0 + n]
+
+        def quantize(tiles, c0, src):
+            codes, scales = mx_cols(tiles, c0, src.shape[1] // PACK)
+            nc.vector.quantize_mx(out=codes, scales=scales, in_=src)
+
+        def mm(acc, lhs, rhs, start, stop):
+            nc.tensor.matmul_mx(out=acc, lhsT=lhs[0], lhsT_scale=lhs[1], rhs=rhs[0], rhs_scale=rhs[1], start=start, stop=stop)
+
+        x_q = [mx_tiles("x%d" % g, PACK * P) for g in range(PASSES)]
+        h_q = [mx_tiles("h%d" % g, R) for g in range(PASSES)]
+        c_q = [mx_tiles("c%d" % b, BANK) for b in range(V // BANK)]
+        z_q = [mx_tiles("z%d" % c, PASSES * W) for c in range(CHUNKS)]
+        x_grp = [keep.tile([P, PACK * P * PACK], BF16, name="x_grp%d" % g, align_bytes=64) for g in range(PASSES)]
+        c_grp = [keep.tile([P, BANK * PACK], BF16, name="c_grp%d" % b, align_bytes=64) for b in range(V // BANK)]
+        h_grp = [keep.tile([P, R * PACK], BF16, name="h_grp%d" % g, align_bytes=64) for g in range(PASSES)]
 
         def turn_x(g, h):
             bank = psum.tile([P, 2, 2, P], F32, name="x_bank", tag="side")
@@ -112,73 +132,59 @@ def tile_diffusion_weighted_refit_s11_kernel(tc, design, coef, basis_words, basi
             x_bank[g, h] = bank
 
         def copy_x(g, h):
-            t = work.tile([P, 2 * P * PACK], BF16, name="x_grp", align_bytes=64, bufs=4)
             nc.scalar.copy(
-                out=t[:].bitcast(F32).rearrange("p (s m u) -> p s m u", s=2, u=2),
+                out=x_grp[g][:, 1024 * h : 1024 * (h + 1)].bitcast(F32).rearrange("p (s m u) -> p s m u", s=2, u=2),
                 in_=x_bank[g, h][:].rearrange("p s u m -> p s m u"),
             )
-            x_grp[g, h] = t
 
-        def quant_x(g, h):
-            x_q[g, h] = quantize(keep, "x%d%d" % (g, h), "x%d%d" % (g, h), x_grp[g, h][:], 1)
+        def quant_x(g, h, n):
+            quantize(x_q[g], 2 * P * h, x_grp[g][:, 1024 * h : 1024 * (h + n)])
 
         def x_slot(g, t):
-            codes, scales = x_q[g, t // 2]
-            cols = slice((t % 2) * P, (t % 2 + 1) * P)
-            return codes[:, cols].bitcast(FP8X4), scales[:, cols]
+            return mx_cols(x_q[g], t * P, P)
 
         def weave_c(c, on_scalar):
-            t = work.tile([P, W * PACK], BF16, name="c_grp", align_bytes=64, bufs=4)
-            dst = t[:].rearrange("p (c i t) -> p c t i", i=RUN, t=PACK)
-            src = c_raw[c].rearrange("p t (c i) -> p c t i", i=RUN)
+            dst = c_grp[c // 2][:, (c % 2) * W * PACK : (c % 2 + 1) * W * PACK].rearrange("p (c i t) -> p c t i", i=RUN, t=PACK)
+            src = window(c_raw, c * W, W).rearrange("p t (c i) -> p c t i", i=RUN)
             if on_scalar:
                 nc.scalar.copy(out=dst, in_=src)
             else:
                 nc.vector.tensor_copy(out=dst, in_=src)
-            c_grp[c] = t
 
-        def quant_c(c):
-            c_q[c] = quantize(keep, "c%d" % c, "c%d" % c, c_grp[c][:], 1)
+        def quant_c(c, n):
+            quantize(c_q[c // 2], (c % 2) * W, c_grp[c // 2][:, (c % 2) * W * PACK : (c % 2 + n) * W * PACK])
 
-        def mm_s(g, c, h):
-            bank = psum.tile([P, 2, W], F32, name="s_bank", tag="s")
-            codes, scales = c_q[c]
-            for s in range(2):
-                xc, xs = x_slot(g, 2 * h + s)
-                nc.tensor.matmul_mx(
-                    out=bank[:, s, :], lhsT=xc, lhsT_scale=xs, rhs=codes[:].bitcast(FP8X4), rhs_scale=scales[:],
-                    start=True, stop=True,
-                )
-            s_bank[g, c, h] = bank
+        def mm_s(g, c):
+            for b in range(2):
+                bank = psum.tile([P, 2, W], F32, name="s_bank", tag="s")
+                for s in range(2):
+                    mm(bank[:, s, :], x_slot(g, 2 * b + s), mx_cols(c_q[c // 2], (c % 2) * W, W), True, True)
+                s_banks[g, c, b] = bank
 
-        def exp_s(g, c, h):
-            if h == 0:
-                e_sb[g, c] = work.tile([P, PACK, W], F32, name="e_sb", bufs=6)
-            nc.scalar.activation(out=e_sb[g, c][:, 2 * h : 2 * h + 2, :], in_=s_bank[g, c, h][:], func=ACT.Exp)
+        def exp_s(g, c):
+            e_sb[g, c] = work.tile([P, PACK, W], F32, name="e_sb", bufs=5)
+            for b in range(2):
+                nc.scalar.activation(out=e_sb[g, c][:, 2 * b : 2 * b + 2, :], in_=s_banks[g, c, b][:], func=ACT.Exp)
 
-        def mult_z(g, c):
-            t = work.tile([P, W * PACK], BF16, name="z_grp", align_bytes=64)
+        def mult_z(g, c, p0=0, pw=W):
+            if c not in z_grp:
+                z_grp[c] = work.tile([P, PASSES * W * PACK], BF16, name="z_grp", align_bytes=64)
+            z0 = (g * W + p0) * PACK
             nc.vector.tensor_tensor(
-                out=t[:].rearrange("p (c i t) -> p c t i", i=RUN, t=PACK),
-                in0=e_sb[g, c][:].rearrange("p t (c i) -> p c t i", i=RUN),
-                in1=y_raw[g, c].rearrange("p t (c i) -> p c t i", i=RUN),
+                out=z_grp[c][:, z0 : z0 + pw * PACK].rearrange("p (c i t) -> p c t i", i=RUN, t=PACK),
+                in0=e_sb[g, c][:, :, p0 : p0 + pw].rearrange("p t (c i) -> p c t i", i=RUN),
+                in1=window(y_raw[g], c * W + p0, pw).rearrange("p t (c i) -> p c t i", i=RUN),
                 op=ALU.mult,
             )
-            z_grp[g, c] = t
 
-        def quant_z(g, c):
-            z_q[g, c] = quantize(work, "z", "z", z_grp[g, c][:], 8)
+        def quant_z(c, z0=0, n=PASSES * W):
+            quantize(z_q[c], z0, z_grp[c][:, z0 * PACK : (z0 + n) * PACK])
 
         def mm_h(g, j):
             bank = psum.tile([P, PACK, P], F32, name="h_bank", tag="side")
             for t in range(PACK):
-                xc, xs = x_slot(g, t)
-                nc.tensor.matmul_mx(
-                    out=bank[:, t, :], lhsT=xc, lhsT_scale=xs,
-                    rhs=u_words[:, 2 * P * j : 2 * P * (j + 1)].bitcast(FP4X4),
-                    rhs_scale=u_scales[:, P * j : P * (j + 1)],
-                    start=True, stop=True,
-                )
+                u = (u_words[:, 2 * P * j : 2 * P * (j + 1)].bitcast(FP4X4), u_scales[:, P * j : P * (j + 1)])
+                mm(bank[:, t, :], x_slot(g, t), u, True, True)
             h_bank[g, j] = bank
 
         def scale_h(g, j):
@@ -190,148 +196,141 @@ def tile_diffusion_weighted_refit_s11_kernel(tc, design, coef, basis_words, basi
             )
 
         def quant_h(g):
-            h_q[g] = quantize(keep, "h%d" % g, "h%d" % g, h_grp[g][:], 1)
+            quantize(h_q[g], 0, h_grp[g][:])
 
-        def mm_o(c):
-            for b in range(2):
-                bank = psum.tile([P, 2, W], F32, name="o_bank", tag="side")
-                for s in range(2):
-                    cols = slice((2 * b + s) * P, (2 * b + s + 1) * P)
+        pending = []
+
+        def mm_o(c, p0=0, w=W):
+            per_bank = BANK // w
+            for b in range(R // P // per_bank):
+                bank = psum.tile([P, per_bank, w], F32, name="o_bank", tag="side")
+                for s in range(per_bank):
                     for g in range(PASSES):
-                        hc, hs = h_q[g]
-                        zc, zs = z_q[g, c]
-                        nc.tensor.matmul_mx(
-                            out=bank[:, s, :], lhsT=hc[:, cols].bitcast(FP8X4), lhsT_scale=hs[:, cols],
-                            rhs=zc[:].bitcast(FP8X4), rhs_scale=zs[:],
-                            start=(g == 0), stop=(g == PASSES - 1),
-                        )
-                o_bank[c, b] = bank
+                        mm(bank[:, s, :], mx_cols(h_q[g], (per_bank * b + s) * P, P), mx_cols(z_q[c], g * W + p0, w), g == 0, g == PASSES - 1)
+                pending.append((bank, per_bank * b, per_bank, c * W + p0, w))
 
-        def store_o(c, b, on_scalar):
-            t = work.tile([P, 2, W], F32, name="o_sb", bufs=4)
-            if on_scalar:
-                nc.scalar.copy(out=t[:], in_=o_bank[c, b][:])
-            else:
-                nc.vector.tensor_copy(out=t[:], in_=o_bank[c, b][:])
-            nc.sync.dma_start(out=out_rows[:, 2 * b : 2 * b + 2, c * W : (c + 1) * W], in_=t[:])
+        def store_o(n):
+            for bank, j0, nj, v0, w in pending[:n]:
+                t = work.tile([P, nj, w], F32, name="o_sb", bufs=8)
+                nc.scalar.copy(out=t[:], in_=bank[:])
+                nc.sync.dma_start(out=out_rows[:, j0 : j0 + nj, v0 : v0 + w], in_=t[:])
+                pending.remove(pending[0])
 
-        def mm_o_last(c, g):
-            for j in range(4):
+        def mm_o_last(c, p0, w, g):
+            for j in range(R // P):
                 if g == 0:
-                    o_bank[c, j] = psum.tile([P, 2, W], F32, name="o_last", tag="s")
-                cols = slice(j * P, (j + 1) * P)
-                hc, hs = h_q[g]
-                zc, zs = z_q[g, c]
-                nc.tensor.matmul_mx(
-                    out=o_bank[c, j][:, 0, :], lhsT=hc[:, cols].bitcast(FP8X4), lhsT_scale=hs[:, cols],
-                    rhs=zc[:].bitcast(FP8X4), rhs_scale=zs[:],
-                    start=(g == 0), stop=(g == PASSES - 1),
-                )
+                    o_bank[j] = psum.tile([P, w], F32, name="o_last", tag="s")
+                mm(o_bank[j][:], mx_cols(h_q[g], j * P, P), mx_cols(z_q[c], g * W + p0, w), g == 0, g == PASSES - 1)
 
-        def store_last(c, b):
-            t = work.tile([P, 2, W], F32, name="o_sb", bufs=4)
-            nc.scalar.copy(out=t[:, 0, :], in_=o_bank[c, 2 * b][:, 0, :])
-            nc.vector.tensor_copy(out=t[:, 1, :], in_=o_bank[c, 2 * b + 1][:, 0, :])
-            nc.sync.dma_start(out=out_rows[:, 2 * b : 2 * b + 2, c * W : (c + 1) * W], in_=t[:])
+        def store_last(v0, w):
+            t = keep.tile([P, R // P, w], F32, name="o_end")
+            for j in range(R // P):
+                nc.vector.tensor_copy(out=t[:, j, :], in_=o_bank[j][:])
+            nc.sync.dma_start(out=out_rows[:, :, v0 : v0 + w], in_=t[:])
+
+        def warm_pe(n):
+            bank = psum.tile([P, PACK, P], F32, name="warm_bank", tag="s")
+            for i in range(n):
+                mm(bank[:, i % PACK, :], mx_cols(zero_q, 0, P), mx_cols(zero_q, 0, P), True, True)
+
+        zero_q = mx_tiles("zero", P)
+        quantize(zero_q, 0, zeros[:])
+        warm_pe(WARM1)
 
         units = [(0, 0), (0, 1), (1, 0), (1, 1)] + [(g, c) for c in range(2, CHUNKS) for g in range(PASSES)]
-
-        def stage_one(k):
-            mm_s(*units[k], 0)
-            mm_s(*units[k], 1)
-
-        def exps(k):
-            exp_s(*units[k], 0)
-            exp_s(*units[k], 1)
+        last = len(units) - 1
 
         turn_x(0, 0)
         copy_x(0, 0)
         turn_x(0, 1)
+        warm_pe(WARM2)
         copy_x(0, 1)
-        quant_x(0, 0)
+        quant_x(0, 0, 1)
         weave_c(0, False)
-        quant_x(0, 1)
-        quant_c(0)
+        quant_x(0, 1, 1)
+        quant_c(0, 1)
         weave_c(1, True)
         mm_h(0, 0)
-        stage_one(0)
-        exps(0)
+        mm_s(*units[0])
         mm_h(0, 1)
-        scale_h(0, 0)
-        quant_c(1)
-        stage_one(1)
-        exps(1)
-        scale_h(0, 1)
         mm_h(0, 2)
+        exp_s(*units[0])
+        scale_h(0, 0)
+        quant_c(1, 1)
+        scale_h(0, 1)
+        mm_s(*units[1])
         mm_h(0, 3)
+        exp_s(*units[1])
+        scale_h(0, 2)
         mult_z(*units[0])
+        scale_h(0, 3)
         turn_x(1, 0)
         turn_x(1, 1)
         copy_x(1, 0)
         copy_x(1, 1)
-        scale_h(0, 2)
-        scale_h(0, 3)
-        quant_z(*units[0])
-        quant_x(1, 0)
-        quant_x(1, 1)
+        mult_z(*units[1])
+        quant_x(1, 0, 2)
+        quant_h(0)
         weave_c(2, True)
-        stage_one(2)
+        weave_c(3, True)
         mm_h(1, 0)
         mm_h(1, 1)
-        stage_one(3)
+        mm_s(*units[2])
         mm_h(1, 2)
+        mm_s(*units[3])
         mm_h(1, 3)
-        exps(2)
-        weave_c(3, True)
-        exps(3)
-        mult_z(*units[1])
-        quant_h(0)
-        quant_c(2)
-        stage_one(4)
+        exp_s(*units[2])
+        exp_s(*units[3])
         scale_h(1, 0)
         scale_h(1, 1)
-        quant_z(*units[1])
+        quant_c(2, 2)
+        mm_s(*units[4])
+        mm_s(*units[5])
         scale_h(1, 2)
         scale_h(1, 3)
         mult_z(*units[2])
         quant_h(1)
-        quant_c(3)
+        exp_s(*units[4])
         weave_c(4, True)
-        exps(4)
-        stage_one(5)
-        quant_z(*units[2])
-
-        last = len(units) - 1
-        pending = []
-        for k in range(3, last):
-            if k + 2 <= last:
-                exps(k + 2)
-            if k + 3 <= last:
-                stage_one(k + 3)
-            if k > 3 and units[k - 1][0] == PASSES - 1:
-                quant_z(*units[k - 1])
-            if units[k - 1][0] == PASSES - 1:
-                mm_o(units[k - 1][1])
-                pending.extend([(units[k - 1][1], 0), (units[k - 1][1], 1)])
-            if k == 3:
-                weave_c(5, True)
-            for n in range(2 if k in (5, 7) else 1):
-                if k > 3:
-                    store_o(*pending[0], True)
-                    pending.remove(pending[0])
-            mult_z(*units[k])
-            if k > 3 and units[k - 1][0] != PASSES - 1:
-                quant_z(*units[k - 1])
-            if k in (3, 5, 7, 9):
-                quant_c(k // 2 + 3)
-            if k in (6, 8):
-                weave_c(k // 2 + 3, False)
-        quant_z(*units[last - 1])
-        mm_o_last(CHUNKS - 1, 0)
-        for c, b in pending:
-            store_o(c, b, True)
-        mult_z(*units[last])
-        quant_z(*units[last])
-        mm_o_last(CHUNKS - 1, 1)
-        store_last(CHUNKS - 1, 0)
-        store_last(CHUNKS - 1, 1)
+        exp_s(*units[5])
+        mm_s(*units[6])
+        weave_c(5, True)
+        quant_z(0)
+        mm_o(0)
+        mult_z(*units[3])
+        for k in range(4, last - 1):
+            g, c = units[k]
+            if k != 10:
+                exp_s(*units[k + 2 if k < 10 else k + 1])
+            store_o(2 if k in (6, 10) else 1)
+            if k != 10:
+                mm_s(*units[k + 3 if k < 10 else k + 2])
+            if g == 1:
+                mm_o(c - 1)
+            mult_z(g, c)
+            if k in (5, 7):
+                weave_c(k // 2 + 4, False)
+            if k == 8:
+                quant_c(6, 2)
+            if k == 4:
+                quant_c(4, 2)
+            if g == 0:
+                quant_z(c - 1)
+        c = CHUNKS - 1
+        exp_s(*units[last])
+        mult_z(0, c, 0, P)
+        quant_z(c - 1)
+        mm_o(c - 1)
+        mult_z(0, c, P, P)
+        mult_z(1, c, 0, P)
+        quant_z(c, 0, W)
+        mm_o_last(c, P, P, 0)
+        quant_z(c, W, P)
+        store_o(len(pending))
+        mm_o(c, 0, P)
+        mult_z(1, c, P, P)
+        quant_z(c, W + P, P)
+        mm_o_last(c, P, P, 1)
+        store_o(1)
+        store_last(c * W + P, P)
+        assert not pending

@@ -22,8 +22,8 @@ PASSES = G // (P * PACK)
 W = 256
 CHUNKS = V // W
 BANK = 512
-WARM1 = 10
-WARM2 = 4
+POPS = (5,)
+SIX = False
 RUN = 4
 
 
@@ -40,13 +40,13 @@ def tile_diffusion_weighted_refit_s11_kernel(tc, design, coef, basis_words, basi
         y_rows = logsig.rearrange("(g p t) v -> g p t v", p=P, t=PACK)
         out_rows = out.rearrange("(j p) v -> p j v", p=P)
 
-        zeros = keep.tile([P, P * PACK], BF16, name="zeros", align_bytes=64)
+        zeros = keep.tile([P, 1], F32, name="zeros")
         warm_out = keep.tile([P, 1], F32, name="warm_out")
 
         u_scales = keep.tile([P, R], U8, name="u_scales", align_bytes=64)
         nc.vector.memset(u_scales[:].bitcast(I32), 0)
         nc.vector.memset(zeros[:], 0.0)
-        nc.scalar.activation(out=warm_out[:], in_=zeros[:, 0:1], func=ACT.Exp)
+        nc.scalar.activation(out=warm_out[:], in_=zeros[:], func=ACT.Exp)
         ident = keep.tile([P, P], F32, name="ident")
         make_identity(nc, ident[:])
         r_sb = keep.tile([P, PASSES, PACK], BF16, name="r_sb")
@@ -78,12 +78,12 @@ def tile_diffusion_weighted_refit_s11_kernel(tc, design, coef, basis_words, basi
         u_words = keep.tile([P, 2 * R], U8, name="u_words", align_bytes=64)
 
         load_x(0, 0, 1)
+        load_x(0, 1, 1)
         for q in range(4):
             nc.sync.dma_start(
                 out=u_scales[32 * q : 32 * q + 4, :].bitcast(I32),
                 in_=basis_scales[0, 4 * q : 4 * q + 4, :].bitcast(I32),
             )
-        load_x(0, 1, 1)
         load_c(0, 256)
         nc.sync.dma_start(out=u_words[:].bitcast(I32), in_=basis_words[0].bitcast(I32))
         load_c(256, 256)
@@ -92,8 +92,8 @@ def tile_diffusion_weighted_refit_s11_kernel(tc, design, coef, basis_words, basi
         load_x(1, 0, 2)
         load_c(512, 512)
         load_y(1, 0, 512)
-        load_y(0, 512, 512)
         load_c(1024, 1024)
+        load_y(0, 512, 512)
         load_y(1, 512, 512)
         load_y(0, 1024, 1024)
         load_y(1, 1024, 1024)
@@ -216,26 +216,18 @@ def tile_diffusion_weighted_refit_s11_kernel(tc, design, coef, basis_words, basi
                 nc.sync.dma_start(out=out_rows[:, j0 : j0 + nj, v0 : v0 + w], in_=t[:])
                 pending.remove(pending[0])
 
-        def mm_o_last(c, p0, w, g):
+        def mm_o_last(c, g):
             for j in range(R // P):
                 if g == 0:
-                    o_bank[j] = psum.tile([P, w], F32, name="o_last", tag="s")
-                mm(o_bank[j][:], mx_cols(h_q[g], j * P, P), mx_cols(z_q[c], g * W + p0, w), g == 0, g == PASSES - 1)
+                    o_bank[j] = psum.tile([P, W], F32, name="o_last", tag="s")
+                mm(o_bank[j][:], mx_cols(h_q[g], j * P, P), mx_cols(z_q[c], g * W, W), g == 0, g == PASSES - 1)
 
-        def store_last(v0, w):
-            t = keep.tile([P, R // P, w], F32, name="o_end")
-            for j in range(R // P):
-                nc.vector.tensor_copy(out=t[:, j, :], in_=o_bank[j][:])
-            nc.sync.dma_start(out=out_rows[:, :, v0 : v0 + w], in_=t[:])
-
-        def warm_pe(n):
-            bank = psum.tile([P, PACK, P], F32, name="warm_bank", tag="s")
-            for i in range(n):
-                mm(bank[:, i % PACK, :], mx_cols(zero_q, 0, P), mx_cols(zero_q, 0, P), True, True)
-
-        zero_q = mx_tiles("zero", P)
-        quantize(zero_q, 0, zeros[:])
-        warm_pe(WARM1)
+        def store_last(c):
+            for b in range(2):
+                t = work.tile([P, 2, W], F32, name="o_sb", bufs=8)
+                nc.vector.tensor_copy(out=t[:, 0, :], in_=o_bank[2 * b][:])
+                nc.scalar.copy(out=t[:, 1, :], in_=o_bank[2 * b + 1][:])
+                nc.sync.dma_start(out=out_rows[:, 2 * b : 2 * b + 2, c * W : (c + 1) * W], in_=t[:])
 
         units = [(0, 0), (0, 1), (1, 0), (1, 1)] + [(g, c) for c in range(2, CHUNKS) for g in range(PASSES)]
         last = len(units) - 1
@@ -243,7 +235,6 @@ def tile_diffusion_weighted_refit_s11_kernel(tc, design, coef, basis_words, basi
         turn_x(0, 0)
         copy_x(0, 0)
         turn_x(0, 1)
-        warm_pe(WARM2)
         copy_x(0, 1)
         quant_x(0, 0, 1)
         weave_c(0, False)
@@ -252,85 +243,82 @@ def tile_diffusion_weighted_refit_s11_kernel(tc, design, coef, basis_words, basi
         weave_c(1, True)
         mm_h(0, 0)
         mm_s(*units[0])
-        mm_h(0, 1)
-        mm_h(0, 2)
         exp_s(*units[0])
+        mm_h(0, 1)
         scale_h(0, 0)
         quant_c(1, 1)
-        scale_h(0, 1)
         mm_s(*units[1])
-        mm_h(0, 3)
         exp_s(*units[1])
-        scale_h(0, 2)
+        scale_h(0, 1)
+        mm_h(0, 2)
+        mm_h(0, 3)
         mult_z(*units[0])
-        scale_h(0, 3)
         turn_x(1, 0)
         turn_x(1, 1)
         copy_x(1, 0)
         copy_x(1, 1)
-        mult_z(*units[1])
-        quant_x(1, 0, 2)
-        quant_h(0)
+        scale_h(0, 2)
+        scale_h(0, 3)
+        quant_x(1, 0, 1)
+        quant_x(1, 1, 1)
         weave_c(2, True)
-        weave_c(3, True)
+        mm_s(*units[2])
         mm_h(1, 0)
         mm_h(1, 1)
-        mm_s(*units[2])
-        mm_h(1, 2)
         mm_s(*units[3])
+        mm_h(1, 2)
         mm_h(1, 3)
         exp_s(*units[2])
+        weave_c(3, True)
         exp_s(*units[3])
+        mult_z(*units[1])
+        quant_h(0)
+        quant_c(2, 1)
+        mm_s(*units[4])
         scale_h(1, 0)
         scale_h(1, 1)
-        quant_c(2, 2)
-        mm_s(*units[4])
-        mm_s(*units[5])
         scale_h(1, 2)
         scale_h(1, 3)
+        quant_c(3, 1)
         mult_z(*units[2])
         quant_h(1)
-        exp_s(*units[4])
         weave_c(4, True)
+        exp_s(*units[4])
+        mm_s(*units[5])
         exp_s(*units[5])
         mm_s(*units[6])
-        weave_c(5, True)
         quant_z(0)
         mm_o(0)
+        weave_c(5, True)
         mult_z(*units[3])
         for k in range(4, last - 1):
             g, c = units[k]
-            if k != 10:
-                exp_s(*units[k + 2 if k < 10 else k + 1])
-            store_o(2 if k in (6, 10) else 1)
-            if k != 10:
-                mm_s(*units[k + 3 if k < 10 else k + 2])
-            if g == 1:
-                mm_o(c - 1)
+            exp_s(*units[k + 2])
+            if k + 3 <= last:
+                mm_s(*units[k + 3])
             mult_z(g, c)
-            if k in (5, 7):
-                weave_c(k // 2 + 4, False)
-            if k == 8:
-                quant_c(6, 2)
             if k == 4:
                 quant_c(4, 2)
             if g == 0:
                 quant_z(c - 1)
+                mm_o(c - 1)
+            store_o(2 if k in POPS else 1)
+            if k == 6:
+                weave_c(6, SIX)
+            if k == 7:
+                weave_c(7, False)
+            if k == 8:
+                quant_c(6, 2)
         c = CHUNKS - 1
-        exp_s(*units[last])
         mult_z(0, c, 0, P)
         quant_z(c - 1)
         mm_o(c - 1)
         mult_z(0, c, P, P)
         mult_z(1, c, 0, P)
         quant_z(c, 0, W)
-        mm_o_last(c, P, P, 0)
-        quant_z(c, W, P)
-        store_o(len(pending))
-        mm_o(c, 0, P)
+        mm_o_last(c, 0)
         mult_z(1, c, P, P)
-        quant_z(c, W + P, P)
-        mm_o_last(c, P, P, 1)
-        store_o(1)
-        store_last(c * W + P, P)
-        assert not pending
+        store_o(len(pending))
+        quant_z(c, W, W)
+        mm_o_last(c, 1)
+        store_last(c)

from contextlib import ExitStack

import concourse.mybir as mybir
from concourse.masks import make_identity

G, K, V, R = 1024, 512, 2048, 512
FLOPS = 2 * G * K * V + 2 * G * K * R + 2 * G * R * V

F32 = mybir.dt.float32
BF16 = mybir.dt.bfloat16
I32 = mybir.dt.int32
U32 = mybir.dt.uint32
U8 = mybir.dt.uint8
FP8X4 = mybir.dt.float8_e4m3fn_x4
FP4X4 = mybir.dt.float4_e2m1fn_x4
ACT = mybir.ActivationFunctionType
ALU = mybir.AluOpType

P = 128
PACK = 4
PASSES = G // (P * PACK)
W = 256
CHUNKS = V // W
BANK = 512
POPS = (5,)
SIX = False
RUN = 4


def tile_diffusion_weighted_refit_s11_kernel(tc, design, coef, basis_words, basis_scales, logsig, prec, out):
    nc = tc.nc
    with ExitStack() as ctx:
        keep = ctx.enter_context(tc.tile_pool(name="keep", bufs=1))
        work = ctx.enter_context(tc.tile_pool(name="work", bufs=3))
        psum = ctx.enter_context(tc.psum_pool(name="psum", bufs=4))
        ctx.enter_context(tc.manual_schedule())

        x_rows = design.rearrange("(g p t) k -> g p t k", p=P, t=PACK)
        c_rows = coef.rearrange("(p t) v -> p t v", t=PACK)
        y_rows = logsig.rearrange("(g p t) v -> g p t v", p=P, t=PACK)
        out_rows = out.rearrange("(j p) v -> p j v", p=P)

        zeros = keep.tile([P, 1], F32, name="zeros")
        warm_out = keep.tile([P, 1], F32, name="warm_out")

        u_scales = keep.tile([P, R], U8, name="u_scales", align_bytes=64)
        nc.vector.memset(u_scales[:].bitcast(I32), 0)
        nc.vector.memset(zeros[:], 0.0)
        nc.scalar.activation(out=warm_out[:], in_=zeros[:], func=ACT.Exp)
        ident = keep.tile([P, P], F32, name="ident")
        make_identity(nc, ident[:])
        r_sb = keep.tile([P, PASSES, PACK], BF16, name="r_sb")

        x_raw, c_raw, y_raw = {}, {}, [{}, {}]

        def load_x(g, h0, n):
            t = keep.tile([P, 2 * n * K], BF16, name="x_raw%d%d" % (g, h0))
            nc.sync.dma_start(out=t[:], in_=x_rows[g, :, 2 * h0 : 2 * (h0 + n), :].rearrange("p t k -> p (t k)"))
            for i in range(n):
                x_raw[g, h0 + i] = t[:, 2 * K * i : 2 * K * (i + 1)]

        def load_c(v0, w):
            t = keep.tile([P, PACK, w], BF16, name="c_raw%d" % v0)
            nc.sync.dma_start(out=t[:], in_=c_rows[:, :, v0 : v0 + w])
            c_raw[v0, v0 + w] = t

        def load_y(g, v0, w):
            t = keep.tile([P, PACK, w], BF16, name="y_raw%d_%d" % (g, v0))
            nc.sync.dma_start(out=t[:], in_=y_rows[g, :, :, v0 : v0 + w])
            y_raw[g][v0, v0 + w] = t

        def window(loaded, v0, w):
            for (lo, hi), t in loaded.items():
                if lo <= v0 and v0 + w <= hi:
                    return t[:, :, v0 - lo : v0 - lo + w]
            raise ValueError("columns not loaded")

        u_words = keep.tile([P, 2 * R], U8, name="u_words", align_bytes=64)

        load_x(0, 0, 1)
        load_x(0, 1, 1)
        for q in range(4):
            nc.sync.dma_start(
                out=u_scales[32 * q : 32 * q + 4, :].bitcast(I32),
                in_=basis_scales[0, 4 * q : 4 * q + 4, :].bitcast(I32),
            )
        load_c(0, 256)
        nc.sync.dma_start(out=u_words[:].bitcast(I32), in_=basis_words[0].bitcast(I32))
        load_c(256, 256)
        nc.sync.dma_start(out=r_sb[:], in_=prec.rearrange("(g p t) -> p g t", p=P, t=PACK))
        load_y(0, 0, 512)
        load_x(1, 0, 2)
        load_c(512, 512)
        load_y(1, 0, 512)
        load_c(1024, 1024)
        load_y(0, 512, 512)
        load_y(1, 512, 512)
        load_y(0, 1024, 1024)
        load_y(1, 1024, 1024)

        x_bank, s_banks, e_sb, z_grp, h_bank, o_bank = {}, {}, {}, {}, {}, {}

        def mx_tiles(name, n):
            codes = keep.tile([P, n], U32, name=name + "_codes", align_bytes=64)
            scales = keep.tile([P, n], U8, name=name + "_scales", align_bytes=64)
            return codes, scales

        def mx_cols(tiles, c0, n):
            return tiles[0][:, c0 : c0 + n].bitcast(FP8X4), tiles[1][:, c0 : c0 + n]

        def quantize(tiles, c0, src):
            codes, scales = mx_cols(tiles, c0, src.shape[1] // PACK)
            nc.vector.quantize_mx(out=codes, scales=scales, in_=src)

        def mm(acc, lhs, rhs, start, stop):
            nc.tensor.matmul_mx(out=acc, lhsT=lhs[0], lhsT_scale=lhs[1], rhs=rhs[0], rhs_scale=rhs[1], start=start, stop=stop)

        x_q = [mx_tiles("x%d" % g, PACK * P) for g in range(PASSES)]
        h_q = [mx_tiles("h%d" % g, R) for g in range(PASSES)]
        c_q = [mx_tiles("c%d" % b, BANK) for b in range(V // BANK)]
        z_q = [mx_tiles("z%d" % c, PASSES * W) for c in range(CHUNKS)]
        x_grp = [keep.tile([P, PACK * P * PACK], BF16, name="x_grp%d" % g, align_bytes=64) for g in range(PASSES)]
        c_grp = [keep.tile([P, BANK * PACK], BF16, name="c_grp%d" % b, align_bytes=64) for b in range(V // BANK)]
        h_grp = [keep.tile([P, R * PACK], BF16, name="h_grp%d" % g, align_bytes=64) for g in range(PASSES)]

        def turn_x(g, h):
            bank = psum.tile([P, 2, 2, P], F32, name="x_bank", tag="side")
            words = x_raw[g, h].bitcast(F32)
            for s in range(2):
                for u in range(2):
                    nc.tensor.transpose(bank[:, s, u, :], words[:, 256 * s + u : 256 * (s + 1) : 2], ident[:])
            x_bank[g, h] = bank

        def copy_x(g, h):
            nc.scalar.copy(
                out=x_grp[g][:, 1024 * h : 1024 * (h + 1)].bitcast(F32).rearrange("p (s m u) -> p s m u", s=2, u=2),
                in_=x_bank[g, h][:].rearrange("p s u m -> p s m u"),
            )

        def quant_x(g, h, n):
            quantize(x_q[g], 2 * P * h, x_grp[g][:, 1024 * h : 1024 * (h + n)])

        def x_slot(g, t):
            return mx_cols(x_q[g], t * P, P)

        def weave_c(c, on_scalar):
            dst = c_grp[c // 2][:, (c % 2) * W * PACK : (c % 2 + 1) * W * PACK].rearrange("p (c i t) -> p c t i", i=RUN, t=PACK)
            src = window(c_raw, c * W, W).rearrange("p t (c i) -> p c t i", i=RUN)
            if on_scalar:
                nc.scalar.copy(out=dst, in_=src)
            else:
                nc.vector.tensor_copy(out=dst, in_=src)

        def quant_c(c, n):
            quantize(c_q[c // 2], (c % 2) * W, c_grp[c // 2][:, (c % 2) * W * PACK : (c % 2 + n) * W * PACK])

        def mm_s(g, c):
            for b in range(2):
                bank = psum.tile([P, 2, W], F32, name="s_bank", tag="s")
                for s in range(2):
                    mm(bank[:, s, :], x_slot(g, 2 * b + s), mx_cols(c_q[c // 2], (c % 2) * W, W), True, True)
                s_banks[g, c, b] = bank

        def exp_s(g, c):
            e_sb[g, c] = work.tile([P, PACK, W], F32, name="e_sb", bufs=5)
            for b in range(2):
                nc.scalar.activation(out=e_sb[g, c][:, 2 * b : 2 * b + 2, :], in_=s_banks[g, c, b][:], func=ACT.Exp)

        def mult_z(g, c, p0=0, pw=W):
            if c not in z_grp:
                z_grp[c] = work.tile([P, PASSES * W * PACK], BF16, name="z_grp", align_bytes=64)
            z0 = (g * W + p0) * PACK
            nc.vector.tensor_tensor(
                out=z_grp[c][:, z0 : z0 + pw * PACK].rearrange("p (c i t) -> p c t i", i=RUN, t=PACK),
                in0=e_sb[g, c][:, :, p0 : p0 + pw].rearrange("p t (c i) -> p c t i", i=RUN),
                in1=window(y_raw[g], c * W + p0, pw).rearrange("p t (c i) -> p c t i", i=RUN),
                op=ALU.mult,
            )

        def quant_z(c, z0=0, n=PASSES * W):
            quantize(z_q[c], z0, z_grp[c][:, z0 * PACK : (z0 + n) * PACK])

        def mm_h(g, j):
            bank = psum.tile([P, PACK, P], F32, name="h_bank", tag="side")
            for t in range(PACK):
                u = (u_words[:, 2 * P * j : 2 * P * (j + 1)].bitcast(FP4X4), u_scales[:, P * j : P * (j + 1)])
                mm(bank[:, t, :], x_slot(g, t), u, True, True)
            h_bank[g, j] = bank

        def scale_h(g, j):
            nc.vector.tensor_tensor(
                out=h_grp[g][:, j * P * PACK : (j + 1) * P * PACK].rearrange("p (n t) -> p n t", t=PACK),
                in0=h_bank[g, j][:].rearrange("p t n -> p n t"),
                in1=r_sb[:, g : g + 1, :].to_broadcast([P, P, PACK]),
                op=ALU.mult,
            )

        def quant_h(g):
            quantize(h_q[g], 0, h_grp[g][:])

        pending = []

        def mm_o(c, p0=0, w=W):
            per_bank = BANK // w
            for b in range(R // P // per_bank):
                bank = psum.tile([P, per_bank, w], F32, name="o_bank", tag="side")
                for s in range(per_bank):
                    for g in range(PASSES):
                        mm(bank[:, s, :], mx_cols(h_q[g], (per_bank * b + s) * P, P), mx_cols(z_q[c], g * W + p0, w), g == 0, g == PASSES - 1)
                pending.append((bank, per_bank * b, per_bank, c * W + p0, w))

        def store_o(n):
            for bank, j0, nj, v0, w in pending[:n]:
                t = work.tile([P, nj, w], F32, name="o_sb", bufs=8)
                nc.scalar.copy(out=t[:], in_=bank[:])
                nc.sync.dma_start(out=out_rows[:, j0 : j0 + nj, v0 : v0 + w], in_=t[:])
                pending.remove(pending[0])

        def mm_o_last(c, g):
            for j in range(R // P):
                if g == 0:
                    o_bank[j] = psum.tile([P, W], F32, name="o_last", tag="s")
                mm(o_bank[j][:], mx_cols(h_q[g], j * P, P), mx_cols(z_q[c], g * W, W), g == 0, g == PASSES - 1)

        def store_last(c):
            for b in range(2):
                t = work.tile([P, 2, W], F32, name="o_sb", bufs=8)
                nc.vector.tensor_copy(out=t[:, 0, :], in_=o_bank[2 * b][:])
                nc.scalar.copy(out=t[:, 1, :], in_=o_bank[2 * b + 1][:])
                nc.sync.dma_start(out=out_rows[:, 2 * b : 2 * b + 2, c * W : (c + 1) * W], in_=t[:])

        units = [(0, 0), (0, 1), (1, 0), (1, 1)] + [(g, c) for c in range(2, CHUNKS) for g in range(PASSES)]
        last = len(units) - 1

        turn_x(0, 0)
        copy_x(0, 0)
        turn_x(0, 1)
        copy_x(0, 1)
        quant_x(0, 0, 1)
        weave_c(0, False)
        quant_x(0, 1, 1)
        quant_c(0, 1)
        weave_c(1, True)
        mm_h(0, 0)
        mm_s(*units[0])
        exp_s(*units[0])
        mm_h(0, 1)
        scale_h(0, 0)
        quant_c(1, 1)
        mm_s(*units[1])
        exp_s(*units[1])
        scale_h(0, 1)
        mm_h(0, 2)
        mm_h(0, 3)
        mult_z(*units[0])
        turn_x(1, 0)
        turn_x(1, 1)
        copy_x(1, 0)
        copy_x(1, 1)
        scale_h(0, 2)
        scale_h(0, 3)
        quant_x(1, 0, 1)
        quant_x(1, 1, 1)
        weave_c(2, True)
        mm_s(*units[2])
        mm_h(1, 0)
        mm_h(1, 1)
        mm_s(*units[3])
        mm_h(1, 2)
        mm_h(1, 3)
        exp_s(*units[2])
        weave_c(3, True)
        exp_s(*units[3])
        mult_z(*units[1])
        quant_h(0)
        quant_c(2, 1)
        mm_s(*units[4])
        scale_h(1, 0)
        scale_h(1, 1)
        scale_h(1, 2)
        scale_h(1, 3)
        quant_c(3, 1)
        mult_z(*units[2])
        quant_h(1)
        weave_c(4, True)
        exp_s(*units[4])
        mm_s(*units[5])
        exp_s(*units[5])
        mm_s(*units[6])
        quant_z(0)
        mm_o(0)
        weave_c(5, True)
        mult_z(*units[3])
        for k in range(4, last - 1):
            g, c = units[k]
            exp_s(*units[k + 2])
            if k + 3 <= last:
                mm_s(*units[k + 3])
            mult_z(g, c)
            if k == 4:
                quant_c(4, 2)
            if g == 0:
                quant_z(c - 1)
                mm_o(c - 1)
            store_o(2 if k in POPS else 1)
            if k == 6:
                weave_c(6, SIX)
            if k == 7:
                weave_c(7, False)
            if k == 8:
                quant_c(6, 2)
        c = CHUNKS - 1
        mult_z(0, c, 0, P)
        quant_z(c - 1)
        mm_o(c - 1)
        mult_z(0, c, P, P)
        mult_z(1, c, 0, P)
        quant_z(c, 0, W)
        mm_o_last(c, 0)
        mult_z(1, c, P, P)
        store_o(len(pending))
        quant_z(c, W, W)
        mm_o_last(c, 1)
        store_last(c)
